import numpy as np
import ml_dtypes


def mxq(x, axis, fmt="e4m3"):
    dtype, down = {"e4m3": (ml_dtypes.float8_e4m3fn, 7), "e5m2": (ml_dtypes.float8_e5m2, 14)}[fmt]
    v = np.moveaxis(np.asarray(x, np.float32).astype(ml_dtypes.bfloat16).astype(np.float64), axis, -1)
    blocks = v.reshape(v.shape[:-1] + (-1, 32))
    amax = np.abs(blocks).max(-1, keepdims=True)
    byte = np.maximum(np.where(amax > 0, np.frexp(amax)[1] - 1 + 127, 0) - down, 1)
    scale = np.exp2(byte - 127.0)
    codes = (blocks / scale).astype(np.float32).astype(dtype).astype(np.float64)
    return np.moveaxis((codes * scale).reshape(v.shape), -1, axis)


WIDE = False


def mx_kscale(k):
    if not WIDE:
        return np.ones(k)
    levels = np.array([10, -10, 5, -5, 0])
    if k % 512:
        return np.exp2(np.random.permutation(np.resize(levels, k // 32))).repeat(32)
    a = np.empty((k // 512, 16))
    for p in range(k // 512):
        a[p, :8] = np.random.permutation(np.resize(levels, 8))
        for g in range(8):
            far = levels[np.abs(levels - a[p, g]) >= 10]
            a[p, g + 8] = far[np.random.randint(len(far))]
    return np.exp2(a.ravel()).repeat(32)


def f64(x):
    return np.asarray(x).astype(np.float64)


def striped(idx):
    return np.tile(idx.reshape(-1, 16).T, (8, 1)).astype(np.uint16)


def unstriped(offs):
    return offs[:16].T.reshape(-1).astype(np.int64)


def pack_weight(w):
    k, n = w.shape
    w = f64(np.asarray(w, np.float32).astype(ml_dtypes.bfloat16)).reshape(k // 32, 32, n)
    amax = np.abs(w).max(1)
    byte = np.clip(np.where(amax > 0, np.frexp(amax)[1] - 1 + 127 - 7, 1), 1, 254)
    scaled = (w * np.exp2(127.0 - byte)[:, None, :]).reshape(k, n).astype(np.float32)
    words = np.ascontiguousarray(scaled.reshape(k // 512, 128, 4, n).transpose(0, 1, 3, 2)).astype(ml_dtypes.float8_e4m3fn).view(np.uint8)
    return words, np.ascontiguousarray(byte.astype(np.uint8).reshape(k // 512, 16, n))


def unpack_weight(words, scales):
    g, p, n, _ = words.shape
    vals = np.ascontiguousarray(words).view(ml_dtypes.float8_e4m3fn).astype(np.float64) * np.repeat(np.exp2(scales.astype(np.float64) - 127.0), 8, axis=1)[..., None]
    return vals.transpose(0, 1, 3, 2).reshape(g * 512, n)


K, T, S, N, U, D = 1024, 2048, 512, 256, 512, 3
P = 2 ** 7


def setup_inputs():
    n = np.random.standard_normal
    s = mx_kscale(K)[:, None]
    packed_xT = pack_weight(n((K, T)) * s)
    return {
        "x_words": packed_xT[0],
        "x_scales": packed_xT[1],
        "w1": (n((K, N)) / np.sqrt(K) / s).astype(np.float32),
        "sign": (np.tile(np.where(np.random.uniform(size=(D, 1, U)) < 0.5, 1.0, -1.0), (1, P, 1))).astype(np.float32),
        "offs": striped(np.random.permutation(T)[:S]),
        "hash1": striped(np.random.randint(0, S, U)),
        "hash2": striped(np.random.randint(0, S, U)),
        "hash3": striped(np.random.randint(0, S, U)),
    }


def reference(x_words, x_scales, w1, sign, offs, hash1, hash2, hash3):
    xq = unpack_weight(x_words, x_scales)[:, unstriped(offs)]
    y = mxq(f64(w1), 0, "e4m3").T @ xq
    g0 = y[:, unstriped(hash1)] * f64(sign)[0, :1]
    g1 = y[:, unstriped(hash2)] * f64(sign)[1, :1]
    g2 = y[:, unstriped(hash3)] * f64(sign)[2, :1]
    return np.maximum(np.minimum(g0, g1), np.minimum(np.maximum(g0, g1), g2))

@@ -1,0 +1,154 @@
+from contextlib import ExitStack
+
+import concourse.mybir as mybir
+
+K, T, S, N, U, D = 1024, 2048, 512, 256, 512, 3
+FLOPS = 2 * K * N * S
+
+F32 = mybir.dt.float32
+BF16 = mybir.dt.bfloat16
+I32 = mybir.dt.int32
+U32 = mybir.dt.uint32
+U16 = mybir.dt.uint16
+U8 = mybir.dt.uint8
+FP8X4 = mybir.dt.float8_e4m3fn_x4
+ALU = mybir.AluOpType
+COPY = mybir.ActivationFunctionType.Copy
+
+P = 128
+PACK = 4
+PASSES = K // (P * PACK)
+BLOCKS = N // P
+HALF = S // 2
+CHUNK = 256
+HI, G0, G2, G1 = 0, 1, 2, 3
+SLOT = (G0, G1, G2)
+
+
+def entries(lst, start, count):
+    return lst[:, start // 16 : (start + count) // 16]
+
+
+def tile_picked_ycsk_med_p_kernel(tc, x_words, x_scales, w1, sign, offs, hash1, hash2, hash3, out):
+    nc = tc.nc
+    with ExitStack() as ctx:
+        keep = ctx.enter_context(tc.tile_pool(name="keep", bufs=1))
+        psum = ctx.enter_context(tc.psum_pool(name="psum", bufs=1))
+
+        picks = keep.tile([P, S // 16], U16, name="picks")
+        nc.sync.dma_start(picks[:], offs)
+
+        scale_table = keep.tile([P, T], U8, name="scale_table")
+        nc.gpsimd.memset(scale_table[:].bitcast(I32), 0)
+        for q in range(4):
+            nc.gpsimd.dma_start(
+                out=scale_table[32 * q : 32 * q + 4 * PASSES, :].bitcast(I32),
+                in_=x_scales[:, 4 * q : 4 * q + 4, :].bitcast(I32),
+            )
+
+        w_raw = []
+        for o in range(PASSES):
+            t = keep.tile([P, PACK, N], F32, name="w_raw%d" % o)
+            nc.sync.dma_start(out=t[:], in_=w1[512 * o : 512 * (o + 1), :].rearrange("(p j) n -> p j n", j=PACK))
+            w_raw.append(t)
+        word_table = []
+        for o in range(PASSES):
+            t = keep.tile([P, T], U32, name="word_table%d" % o)
+            nc.sync.dma_start(out=t[:].bitcast(I32), in_=x_words[o].rearrange("p c r -> p (c r)").bitcast(I32))
+            word_table.append(t)
+        hashes = []
+        for d, src in enumerate((hash1, hash2, hash3)):
+            t = keep.tile([P, U // 16], U16, name="hash_list%d" % d)
+            nc.sync.dma_start(t[:], src)
+            hashes.append(t)
+        signs = keep.tile([P, D, U], F32, name="signs")
+        nc.sync.dma_start(out=signs[:], in_=sign.rearrange("d p r -> p d r"))
+
+        x_planes = keep.tile([P, S], U8, name="x_planes", align_bytes=64)
+        nc.vector.tensor_copy(x_planes[:], scale_table[:].indirect(picks[:]))
+
+        w_codes, w_planes = [], []
+        for o in range(PASSES):
+            grouped = keep.tile([P, N, PACK], BF16, name="w_grouped%d" % o, align_bytes=64)
+            nc.scalar.copy(
+                out=grouped[:].rearrange("p (c i) j -> p c j i", i=4),
+                in_=w_raw[o][:].rearrange("p j (c i) -> p c j i", i=4),
+            )
+            codes = keep.tile([P, N], U32, name="w_codes%d" % o, align_bytes=64)
+            plane = keep.tile([P, N], U8, name="w_plane%d" % o, align_bytes=64)
+            nc.vector.quantize_mx(out=codes[:].bitcast(FP8X4), scales=plane[:], in_=grouped[:].rearrange("p n j -> p (n j)"))
+            w_codes.append(codes)
+            w_planes.append(plane)
+
+        x_codes = [keep.tile([P, S], U32, name="x_codes%d" % o, align_bytes=64) for o in range(PASSES)]
+        acc = [[psum.tile([P, HALF], F32, name="acc%d%d" % (b, h)) for h in range(2)] for b in range(BLOCKS)]
+        y = [keep.tile([P, S], F32, name="y%d" % b) for b in range(BLOCKS)]
+
+        def multiply(o, h):
+            cols = slice(h * HALF, (h + 1) * HALF)
+            for b in range(BLOCKS):
+                rows = slice(b * P, (b + 1) * P)
+                nc.tensor.matmul_mx(
+                    out=acc[b][h][:],
+                    lhsT=w_codes[o][:, rows].bitcast(FP8X4),
+                    lhsT_scale=w_planes[o][:, rows],
+                    rhs=x_codes[o][:, cols].bitcast(FP8X4),
+                    rhs_scale=x_planes[4 * o : P, cols],
+                    start=(o == 0),
+                    stop=(o == PASSES - 1),
+                )
+
+        nc.vector.tensor_copy(x_codes[0][:], word_table[0][:].indirect(picks[:]))
+        multiply(0, 0)
+        multiply(0, 1)
+        for h in range(2):
+            cols = slice(h * HALF, (h + 1) * HALF)
+            nc.vector.tensor_copy(x_codes[1][:, cols], word_table[1][:].indirect(entries(picks, h * HALF, HALF)))
+            multiply(1, h)
+        for b in range(BLOCKS):
+            nc.scalar.copy(out=y[b][:, :HALF], in_=acc[b][0][:])
+        nc.vector.tensor_copy(out=y[0][:, HALF:], in_=acc[0][1][:])
+
+        chunks = [(b, r0) for b in range(BLOCKS) for r0 in range(0, U, CHUNK)]
+        work = [keep.tile([P, 4, CHUNK], F32, name="work%d" % c) for c in range(len(chunks))]
+        low = [keep.tile([P, 2, CHUNK], F32, name="low%d" % c) for c in range(len(chunks))]
+        res = [keep.tile([P, CHUNK], F32, name="res%d" % c) for c in range(len(chunks))]
+
+        def signed(c, d):
+            b, r0 = chunks[c]
+            window = y[b][:].indirect(entries(hashes[d], r0, CHUNK))
+            g = work[c][:, SLOT[d], :]
+            s = signs[:, d, r0 : r0 + CHUNK]
+            if c == 0 and d == 0:
+                nc.vector.tensor_tensor(g, window, s, ALU.mult)
+            else:
+                nc.scalar.activation(g, window, COPY)
+                nc.vector.tensor_tensor(g, g, s, ALU.mult)
+
+        def upper(c, cols):
+            nc.vector.tensor_tensor(work[c][:, HI, cols], work[c][:, G0, cols], work[c][:, G1, cols], ALU.max)
+
+        def lower(c, cols):
+            nc.vector.tensor_tensor(low[c][:, :, cols], work[c][:, HI : G0 + 1, cols], work[c][:, G2 : G1 + 1, cols], ALU.min)
+
+        def middle(c, cols):
+            b, r0 = chunks[c]
+            nc.vector.tensor_tensor(res[c][:, cols], low[c][:, 0, cols], low[c][:, 1, cols], ALU.max)
+            nc.sync.dma_start(out=out[b * P : (b + 1) * P, r0 + cols.start : r0 + cols.stop], in_=res[c][:, cols])
+
+        whole = slice(0, CHUNK)
+        signed(0, 0)
+        signed(0, 1)
+        nc.vector.tensor_copy(out=y[1][:, HALF:], in_=acc[1][1][:])
+        signed(0, 2)
+        for c in range(len(chunks) - 1):
+            upper(c, whole)
+            signed(c + 1, 0)
+            lower(c, whole)
+            signed(c + 1, 1)
+            middle(c, whole)
+            signed(c + 1, 2)
+        halves = (slice(0, CHUNK // 2), slice(CHUNK // 2, CHUNK))
+        for step in (upper, lower, middle):
+            for cols in halves:
+                step(len(chunks) - 1, cols)

@@ -19,7 +19,7 @@ P = 128
 PACK = 4
 PASSES = K // (P * PACK)
 BLOCKS = N // P
-HALF = S // 2
+PIECES = (slice(0, 256), slice(256, 384), slice(384, 512))
 CHUNK = 256
 HI, G0, G2, G1 = 0, 1, 2, 3
 SLOT = (G0, G1, G2)
@@ -35,79 +35,104 @@ def tile_picked_ycsk_med_p_kernel(tc, x_words, x_scales, w1, sign, offs, hash1, 
         keep = ctx.enter_context(tc.tile_pool(name="keep", bufs=1))
         psum = ctx.enter_context(tc.psum_pool(name="psum", bufs=1))
 
-        picks = keep.tile([P, S // 16], U16, name="picks")
-        nc.sync.dma_start(picks[:], offs)
-
-        scale_table = keep.tile([P, T], U8, name="scale_table")
-        nc.gpsimd.memset(scale_table[:].bitcast(I32), 0)
+        scale_rows = keep.tile([P, T], U8, name="scale_rows")
         for q in range(4):
-            nc.gpsimd.dma_start(
-                out=scale_table[32 * q : 32 * q + 4 * PASSES, :].bitcast(I32),
+            nc.sync.dma_start(
+                out=scale_rows[32 * q : 32 * q + 4 * PASSES, :].bitcast(I32),
                 in_=x_scales[:, 4 * q : 4 * q + 4, :].bitcast(I32),
             )
+        scale_table = keep.tile([P, T], U8, name="scale_table")
+        nc.vector.memset(scale_table[:].bitcast(I32), 0)
+        for q in range(4):
+            live = slice(32 * q, 32 * q + 4 * PASSES)
+            nc.vector.tensor_copy(scale_table[live, :].bitcast(I32), scale_rows[live, :].bitcast(I32))
 
-        w_raw = []
-        for o in range(PASSES):
-            t = keep.tile([P, PACK, N], F32, name="w_raw%d" % o)
-            nc.sync.dma_start(out=t[:], in_=w1[512 * o : 512 * (o + 1), :].rearrange("(p j) n -> p j n", j=PACK))
-            w_raw.append(t)
-        word_table = []
-        for o in range(PASSES):
-            t = keep.tile([P, T], U32, name="word_table%d" % o)
-            nc.sync.dma_start(out=t[:].bitcast(I32), in_=x_words[o].rearrange("p c r -> p (c r)").bitcast(I32))
-            word_table.append(t)
+        word_table = [keep.tile([P, T], U32, name="word_table%d" % o) for o in range(PASSES)]
+        picks = keep.tile([P, S // 16], U16, name="picks")
+        w_raw = {}
+
+        def load_weights(o, cols):
+            t = keep.tile([P, PACK, cols.stop - cols.start], F32, name="w_raw%d_%d" % (o, cols.start))
+            nc.sync.dma_start(out=t[:], in_=w1[512 * o : 512 * (o + 1), cols].rearrange("(p j) n -> p j n", j=PACK))
+            w_raw.setdefault((o, cols.start), t)
+
+        def load_words(o):
+            nc.sync.dma_start(out=word_table[o][:].bitcast(I32), in_=x_words[o].rearrange("p c r -> p (c r)").bitcast(I32))
+
+        load_weights(0, slice(0, N))
+        nc.sync.dma_start(picks[:], offs)
+        load_weights(1, slice(0, P))
+        load_words(0)
+        load_words(1)
+        load_weights(1, slice(P, N))
         hashes = []
         for d, src in enumerate((hash1, hash2, hash3)):
             t = keep.tile([P, U // 16], U16, name="hash_list%d" % d)
             nc.sync.dma_start(t[:], src)
             hashes.append(t)
-        signs = keep.tile([P, D, U], F32, name="signs")
-        nc.sync.dma_start(out=signs[:], in_=sign.rearrange("d p r -> p d r"))
+        signs = {}
+        for r0 in range(0, U, CHUNK):
+            t = keep.tile([P, D, CHUNK], F32, name="signs%d" % r0)
+            nc.sync.dma_start(out=t[:], in_=sign[:, :, r0 : r0 + CHUNK].rearrange("d p r -> p d r"))
+            signs.setdefault(r0, t)
 
         x_planes = keep.tile([P, S], U8, name="x_planes", align_bytes=64)
         nc.vector.tensor_copy(x_planes[:], scale_table[:].indirect(picks[:]))
 
-        w_codes, w_planes = [], []
-        for o in range(PASSES):
-            grouped = keep.tile([P, N, PACK], BF16, name="w_grouped%d" % o, align_bytes=64)
-            nc.scalar.copy(
-                out=grouped[:].rearrange("p (c i) j -> p c j i", i=4),
-                in_=w_raw[o][:].rearrange("p j (c i) -> p c j i", i=4),
+        w_codes = [keep.tile([P, N], U32, name="w_codes%d" % o, align_bytes=64) for o in range(PASSES)]
+        w_planes = [keep.tile([P, N], U8, name="w_plane%d" % o, align_bytes=64) for o in range(PASSES)]
+        w_grouped = {}
+
+        def interleave(o, cols):
+            grouped = keep.tile([P, cols.stop - cols.start, PACK], BF16, name="w_grouped%d_%d" % (o, cols.start), align_bytes=64)
+            dst = grouped[:].rearrange("p (c i) j -> p c j i", i=4)
+            src = w_raw[o, cols.start][:].rearrange("p j (c i) -> p c j i", i=4)
+            if cols.start == 0:
+                nc.scalar.copy(out=dst, in_=src)
+            else:
+                nc.vector.tensor_copy(out=dst, in_=src)
+            w_grouped.setdefault((o, cols.start), grouped)
+
+        def quantize(o, cols):
+            nc.vector.quantize_mx(
+                out=w_codes[o][:, cols].bitcast(FP8X4),
+                scales=w_planes[o][:, cols],
+                in_=w_grouped[o, cols.start][:].rearrange("p n j -> p (n j)"),
             )
-            codes = keep.tile([P, N], U32, name="w_codes%d" % o, align_bytes=64)
-            plane = keep.tile([P, N], U8, name="w_plane%d" % o, align_bytes=64)
-            nc.vector.quantize_mx(out=codes[:].bitcast(FP8X4), scales=plane[:], in_=grouped[:].rearrange("p n j -> p (n j)"))
-            w_codes.append(codes)
-            w_planes.append(plane)
 
         x_codes = [keep.tile([P, S], U32, name="x_codes%d" % o, align_bytes=64) for o in range(PASSES)]
-        acc = [[psum.tile([P, HALF], F32, name="acc%d%d" % (b, h)) for h in range(2)] for b in range(BLOCKS)]
         y = [keep.tile([P, S], F32, name="y%d" % b) for b in range(BLOCKS)]
+        first = [psum.tile([P, cols.stop - cols.start], F32, name="first%d" % i) for i, cols in enumerate(PIECES)]
+        second = psum.tile([P, S], F32, name="second")
 
-        def multiply(o, h):
-            cols = slice(h * HALF, (h + 1) * HALF)
-            for b in range(BLOCKS):
-                rows = slice(b * P, (b + 1) * P)
-                nc.tensor.matmul_mx(
-                    out=acc[b][h][:],
-                    lhsT=w_codes[o][:, rows].bitcast(FP8X4),
-                    lhsT_scale=w_planes[o][:, rows],
-                    rhs=x_codes[o][:, cols].bitcast(FP8X4),
-                    rhs_scale=x_planes[4 * o : P, cols],
-                    start=(o == 0),
-                    stop=(o == PASSES - 1),
-                )
+        def multiply(acc, o, b, cols):
+            rows = slice(b * P, (b + 1) * P)
+            nc.tensor.matmul_mx(
+                out=acc[:],
+                lhsT=w_codes[o][:, rows].bitcast(FP8X4),
+                lhsT_scale=w_planes[o][:, rows],
+                rhs=x_codes[o][:, cols].bitcast(FP8X4),
+                rhs_scale=x_planes[4 * o : P, cols],
+                start=(o == 0),
+                stop=(o == PASSES - 1),
+            )
 
+        everything = slice(0, S)
+        for o, cols in ((0, slice(0, N)), (1, slice(0, P))):
+            interleave(o, cols)
+            quantize(o, cols)
         nc.vector.tensor_copy(x_codes[0][:], word_table[0][:].indirect(picks[:]))
-        multiply(0, 0)
-        multiply(0, 1)
-        for h in range(2):
-            cols = slice(h * HALF, (h + 1) * HALF)
-            nc.vector.tensor_copy(x_codes[1][:, cols], word_table[1][:].indirect(entries(picks, h * HALF, HALF)))
-            multiply(1, h)
-        for b in range(BLOCKS):
-            nc.scalar.copy(out=y[b][:, :HALF], in_=acc[b][0][:])
-        nc.vector.tensor_copy(out=y[0][:, HALF:], in_=acc[0][1][:])
+        for acc, cols in zip(first, PIECES):
+            multiply(acc, 0, 0, cols)
+        multiply(second, 0, 1, everything)
+        for acc, cols in zip(first, PIECES):
+            nc.vector.tensor_copy(x_codes[1][:, cols], word_table[1][:].indirect(entries(picks, cols.start, cols.stop - cols.start)))
+            multiply(acc, 1, 0, cols)
+        interleave(1, slice(P, N))
+        quantize(1, slice(P, N))
+        multiply(second, 1, 1, everything)
+        for acc, cols in zip(first, PIECES):
+            nc.scalar.copy(out=y[0][:, cols], in_=acc[:])
 
         chunks = [(b, r0) for b in range(BLOCKS) for r0 in range(0, U, CHUNK)]
         work = [keep.tile([P, 4, CHUNK], F32, name="work%d" % c) for c in range(len(chunks))]
@@ -118,12 +143,13 @@ def tile_picked_ycsk_med_p_kernel(tc, x_words, x_scales, w1, sign, offs, hash1, 
             b, r0 = chunks[c]
             window = y[b][:].indirect(entries(hashes[d], r0, CHUNK))
             g = work[c][:, SLOT[d], :]
-            s = signs[:, d, r0 : r0 + CHUNK]
+            s = signs[r0][:, d, :]
             if c == 0 and d == 0:
                 nc.vector.tensor_tensor(g, window, s, ALU.mult)
             else:
-                nc.scalar.activation(g, window, COPY)
-                nc.vector.tensor_tensor(g, g, s, ALU.mult)
+                raw = keep.tile([P, CHUNK], F32, name="raw%d" % d)
+                nc.scalar.activation(raw[:], window, COPY)
+                nc.vector.tensor_tensor(g, raw[:], s, ALU.mult)
 
         def upper(c, cols):
             nc.vector.tensor_tensor(work[c][:, HI, cols], work[c][:, G0, cols], work[c][:, G1, cols], ALU.max)
@@ -139,9 +165,10 @@ def tile_picked_ycsk_med_p_kernel(tc, x_words, x_scales, w1, sign, offs, hash1, 
         whole = slice(0, CHUNK)
         signed(0, 0)
         signed(0, 1)
-        nc.vector.tensor_copy(out=y[1][:, HALF:], in_=acc[1][1][:])
         signed(0, 2)
         for c in range(len(chunks) - 1):
+            if chunks[c + 1] == (1, 0):
+                nc.scalar.copy(out=y[1][:], in_=second[:])
             upper(c, whole)
             signed(c + 1, 0)
             lower(c, whole)

from contextlib import ExitStack

import concourse.mybir as mybir

K, T, S, N, U, D = 1024, 2048, 512, 256, 512, 3
FLOPS = 2 * K * N * S

F32 = mybir.dt.float32
BF16 = mybir.dt.bfloat16
I32 = mybir.dt.int32
U32 = mybir.dt.uint32
U16 = mybir.dt.uint16
U8 = mybir.dt.uint8
FP8X4 = mybir.dt.float8_e4m3fn_x4
ALU = mybir.AluOpType
COPY = mybir.ActivationFunctionType.Copy

P = 128
PACK = 4
PASSES = K // (P * PACK)
BLOCKS = N // P
PIECES = (slice(0, 256), slice(256, 384), slice(384, 512))
CHUNK = 256
HI, G0, G2, G1 = 0, 1, 2, 3
SLOT = (G0, G1, G2)


def entries(lst, start, count):
    return lst[:, start // 16 : (start + count) // 16]


def tile_picked_ycsk_med_p_kernel(tc, x_words, x_scales, w1, sign, offs, hash1, hash2, hash3, out):
    nc = tc.nc
    with ExitStack() as ctx:
        keep = ctx.enter_context(tc.tile_pool(name="keep", bufs=1))
        psum = ctx.enter_context(tc.psum_pool(name="psum", bufs=1))

        scale_rows = keep.tile([P, T], U8, name="scale_rows")
        for q in range(4):
            nc.sync.dma_start(
                out=scale_rows[32 * q : 32 * q + 4 * PASSES, :].bitcast(I32),
                in_=x_scales[:, 4 * q : 4 * q + 4, :].bitcast(I32),
            )
        scale_table = keep.tile([P, T], U8, name="scale_table")
        nc.vector.memset(scale_table[:].bitcast(I32), 0)
        for q in range(4):
            live = slice(32 * q, 32 * q + 4 * PASSES)
            nc.vector.tensor_copy(scale_table[live, :].bitcast(I32), scale_rows[live, :].bitcast(I32))

        word_table = [keep.tile([P, T], U32, name="word_table%d" % o) for o in range(PASSES)]
        picks = keep.tile([P, S // 16], U16, name="picks")
        w_raw = {}

        def load_weights(o, cols):
            t = keep.tile([P, PACK, cols.stop - cols.start], F32, name="w_raw%d_%d" % (o, cols.start))
            nc.sync.dma_start(out=t[:], in_=w1[512 * o : 512 * (o + 1), cols].rearrange("(p j) n -> p j n", j=PACK))
            w_raw.setdefault((o, cols.start), t)

        def load_words(o):
            nc.sync.dma_start(out=word_table[o][:].bitcast(I32), in_=x_words[o].rearrange("p c r -> p (c r)").bitcast(I32))

        load_weights(0, slice(0, N))
        nc.sync.dma_start(picks[:], offs)
        load_weights(1, slice(0, P))
        load_words(0)
        load_words(1)
        load_weights(1, slice(P, N))
        hashes = []
        for d, src in enumerate((hash1, hash2, hash3)):
            t = keep.tile([P, U // 16], U16, name="hash_list%d" % d)
            nc.sync.dma_start(t[:], src)
            hashes.append(t)
        signs = {}
        for r0 in range(0, U, CHUNK):
            t = keep.tile([P, D, CHUNK], F32, name="signs%d" % r0)
            nc.sync.dma_start(out=t[:], in_=sign[:, :, r0 : r0 + CHUNK].rearrange("d p r -> p d r"))
            signs.setdefault(r0, t)

        x_planes = keep.tile([P, S], U8, name="x_planes", align_bytes=64)
        nc.vector.tensor_copy(x_planes[:], scale_table[:].indirect(picks[:]))

        w_codes = [keep.tile([P, N], U32, name="w_codes%d" % o, align_bytes=64) for o in range(PASSES)]
        w_planes = [keep.tile([P, N], U8, name="w_plane%d" % o, align_bytes=64) for o in range(PASSES)]
        w_grouped = {}

        def interleave(o, cols):
            grouped = keep.tile([P, cols.stop - cols.start, PACK], BF16, name="w_grouped%d_%d" % (o, cols.start), align_bytes=64)
            dst = grouped[:].rearrange("p (c i) j -> p c j i", i=4)
            src = w_raw[o, cols.start][:].rearrange("p j (c i) -> p c j i", i=4)
            if cols.start == 0:
                nc.scalar.copy(out=dst, in_=src)
            else:
                nc.vector.tensor_copy(out=dst, in_=src)
            w_grouped.setdefault((o, cols.start), grouped)

        def quantize(o, cols):
            nc.vector.quantize_mx(
                out=w_codes[o][:, cols].bitcast(FP8X4),
                scales=w_planes[o][:, cols],
                in_=w_grouped[o, cols.start][:].rearrange("p n j -> p (n j)"),
            )

        x_codes = [keep.tile([P, S], U32, name="x_codes%d" % o, align_bytes=64) for o in range(PASSES)]
        y = [keep.tile([P, S], F32, name="y%d" % b) for b in range(BLOCKS)]
        first = [psum.tile([P, cols.stop - cols.start], F32, name="first%d" % i) for i, cols in enumerate(PIECES)]
        second = psum.tile([P, S], F32, name="second")

        def multiply(acc, o, b, cols):
            rows = slice(b * P, (b + 1) * P)
            nc.tensor.matmul_mx(
                out=acc[:],
                lhsT=w_codes[o][:, rows].bitcast(FP8X4),
                lhsT_scale=w_planes[o][:, rows],
                rhs=x_codes[o][:, cols].bitcast(FP8X4),
                rhs_scale=x_planes[4 * o : P, cols],
                start=(o == 0),
                stop=(o == PASSES - 1),
            )

        everything = slice(0, S)
        for o, cols in ((0, slice(0, N)), (1, slice(0, P))):
            interleave(o, cols)
            quantize(o, cols)
        nc.vector.tensor_copy(x_codes[0][:], word_table[0][:].indirect(picks[:]))
        for acc, cols in zip(first, PIECES):
            multiply(acc, 0, 0, cols)
        multiply(second, 0, 1, everything)
        for acc, cols in zip(first, PIECES):
            nc.vector.tensor_copy(x_codes[1][:, cols], word_table[1][:].indirect(entries(picks, cols.start, cols.stop - cols.start)))
            multiply(acc, 1, 0, cols)
        interleave(1, slice(P, N))
        quantize(1, slice(P, N))
        multiply(second, 1, 1, everything)
        for acc, cols in zip(first, PIECES):
            nc.scalar.copy(out=y[0][:, cols], in_=acc[:])

        chunks = [(b, r0) for b in range(BLOCKS) for r0 in range(0, U, CHUNK)]
        work = [keep.tile([P, 4, CHUNK], F32, name="work%d" % c) for c in range(len(chunks))]
        low = [keep.tile([P, 2, CHUNK], F32, name="low%d" % c) for c in range(len(chunks))]
        res = [keep.tile([P, CHUNK], F32, name="res%d" % c) for c in range(len(chunks))]

        def signed(c, d):
            b, r0 = chunks[c]
            window = y[b][:].indirect(entries(hashes[d], r0, CHUNK))
            g = work[c][:, SLOT[d], :]
            s = signs[r0][:, d, :]
            if c == 0 and d == 0:
                nc.vector.tensor_tensor(g, window, s, ALU.mult)
            else:
                raw = keep.tile([P, CHUNK], F32, name="raw%d" % d)
                nc.scalar.activation(raw[:], window, COPY)
                nc.vector.tensor_tensor(g, raw[:], s, ALU.mult)

        def upper(c, cols):
            nc.vector.tensor_tensor(work[c][:, HI, cols], work[c][:, G0, cols], work[c][:, G1, cols], ALU.max)

        def lower(c, cols):
            nc.vector.tensor_tensor(low[c][:, :, cols], work[c][:, HI : G0 + 1, cols], work[c][:, G2 : G1 + 1, cols], ALU.min)

        def middle(c, cols):
            b, r0 = chunks[c]
            nc.vector.tensor_tensor(res[c][:, cols], low[c][:, 0, cols], low[c][:, 1, cols], ALU.max)
            nc.sync.dma_start(out=out[b * P : (b + 1) * P, r0 + cols.start : r0 + cols.stop], in_=res[c][:, cols])

        whole = slice(0, CHUNK)
        signed(0, 0)
        signed(0, 1)
        signed(0, 2)
        for c in range(len(chunks) - 1):
            if chunks[c + 1] == (1, 0):
                nc.scalar.copy(out=y[1][:], in_=second[:])
            upper(c, whole)
            signed(c + 1, 0)
            lower(c, whole)
            signed(c + 1, 1)
            middle(c, whole)
            signed(c + 1, 2)
        halves = (slice(0, CHUNK // 2), slice(CHUNK // 2, CHUNK))
        for step in (upper, lower, middle):
            for cols in halves:
                step(len(chunks) - 1, cols)
